import numpy as np, ml_dtypes
CORES = [8,9,10,11,12,13,14,15,16,17,18,19,20,21,22,23]
N = 16
GROUPS = [[0,1,2,3],[4,5,6,7],[8,9,10,11],[12,13,14,15]]
def setup_inputs(rng):
    return {"x": rng.standard_normal((N, 128, 8), dtype=np.float32).astype(ml_dtypes.bfloat16)}
def reference(x):
    y = np.empty((N, 128, 2), x.dtype)
    for g in GROUPS:
        s = x[g].sum(axis=0, dtype=np.float64).astype(x[g].dtype)
        n = len(g); b = x.shape[2] // n
        for i, r in enumerate(g):
            y[r] = s[:, i * b:(i + 1) * b]
    return {"y": y}

@@ -1,0 +1,46 @@
+from concourse.bass import DstId, RemoteDMATransfer
+from concourse.mybir import AluOpType
+
+SCRATCH = {
+    "xs": ("sbuf", [128, 8], "bfloat16"),
+    "land": ("sbuf", [128, 8], "bfloat16"),
+}
+SEMAPHORES = ["loaded", "own", "read", "arrived", "local"]
+
+
+def rank_program(g, core, T, topo):
+    rank = T.rank_of(core)
+    if rank is None:
+        return
+    group = [grp for grp in T.tables["GROUPS"] if rank in grp][0]
+    n = len(group)
+    i = group.index(rank)
+    b = T.x.shape[1] // n
+    s = T.sem
+
+    g.sync.dma_start(T.xs[:], T.x[:]).then_inc(s.loaded, 16)
+    g.scalar.dma_start(T.land[:, i * b:(i + 1) * b], T.x[:, i * b:(i + 1) * b]).then_inc(s.own, 16)
+
+    g.wait_ge(s.loaded, 16)
+    transfers = []
+    k = 0
+    for j in range(n):
+        if j == i:
+            continue
+        rid, pid, _se = topo.addr(T.cores[group[j]])
+        transfers.append(RemoteDMATransfer(
+            dst_ids=[DstId(rid=rid, pnc=pid)], dma_engine_mask=0xF << (4 * k), remote_sem=s.arrived,
+            src=T.xs[:, j * b:(j + 1) * b], dst=T.land[:, i * b:(i + 1) * b]))
+        k += 1
+    g.remote_dma_fused(transfers, local_sem=s.read)
+
+    g.wait_ge(s.arrived, 4 * (n - 1))
+    g.wait_ge(s.own, 16)
+    g.dma_start(T.land[:, 0:2 * b], T.land[:, 2 * b:4 * b], accum_op=AluOpType.add).then_inc(s.local, 16)
+    g.wait_ge(s.local, 16)
+    g.dma_start(T.land[:, 0:b], T.land[:, b:2 * b], accum_op=AluOpType.add).then_inc(s.local, 16)
+    g.wait_ge(s.local, 32)
+
+    g.dma_start(T.y[:], T.land[:, 0:b]).then_inc(s.local, 16)
+    g.wait_ge(s.local, 48)
+    g.wait_ge(s.read, 4 * (n - 1))

@@ -1,46 +1,45 @@
 from concourse.bass import DstId, RemoteDMATransfer
-from concourse.mybir import AluOpType
 
 SCRATCH = {
-    "xs": ("sbuf", [128, 8], "bfloat16"),
-    "land": ("sbuf", [128, 8], "bfloat16"),
+    "xd": ("dram", [4, 128, 2], "bfloat16"),
+    "land": ("dram", [4, 128, 2], "bfloat16"),
+    "sd": ("dram", [4, 128, 2], "bfloat16"),
 }
-SEMAPHORES = ["loaded", "own", "read", "arrived", "local"]
+SEMAPHORES = ["loaded", "read", "arrived", "done", "stored"]
 
 
 def rank_program(g, core, T, topo):
     rank = T.rank_of(core)
     if rank is None:
         return
-    group = [grp for grp in T.tables["GROUPS"] if rank in grp][0]
+    groups = T.tables["GROUPS"]
+    group = [grp for grp in groups if rank in grp][0]
     n = len(group)
     i = group.index(rank)
-    b = T.x.shape[1] // n
+    partner = [grp for grp in groups
+               if grp is not group and topo.chip(T.cores[grp[0]]) == topo.chip(core)][0]
     s = T.sem
 
-    g.sync.dma_start(T.xs[:], T.x[:]).then_inc(s.loaded, 16)
-    g.scalar.dma_start(T.land[:, i * b:(i + 1) * b], T.x[:, i * b:(i + 1) * b]).then_inc(s.own, 16)
+    def dst_id(member):
+        rid, pid, _se = topo.addr(T.cores[partner[member]])
+        return DstId(rid=rid, pnc=pid)
 
+    g.sync.dma_start(T.xd[:], T.x[:]).then_inc(s.loaded, 16)
     g.wait_ge(s.loaded, 16)
-    transfers = []
-    k = 0
-    for j in range(n):
-        if j == i:
-            continue
-        rid, pid, _se = topo.addr(T.cores[group[j]])
-        transfers.append(RemoteDMATransfer(
-            dst_ids=[DstId(rid=rid, pnc=pid)], dma_engine_mask=0xF << (4 * k), remote_sem=s.arrived,
-            src=T.xs[:, j * b:(j + 1) * b], dst=T.land[:, i * b:(i + 1) * b]))
-        k += 1
-    g.remote_dma_fused(transfers, local_sem=s.read)
 
-    g.wait_ge(s.arrived, 4 * (n - 1))
-    g.wait_ge(s.own, 16)
-    g.dma_start(T.land[:, 0:2 * b], T.land[:, 2 * b:4 * b], accum_op=AluOpType.add).then_inc(s.local, 16)
-    g.wait_ge(s.local, 16)
-    g.dma_start(T.land[:, 0:b], T.land[:, b:2 * b], accum_op=AluOpType.add).then_inc(s.local, 16)
-    g.wait_ge(s.local, 32)
+    g.remote_dma_fused(
+        [RemoteDMATransfer(dst_ids=[dst_id(m)], dma_engine_mask=0xF << (4 * m), remote_sem=s.arrived,
+                           src=T.xd[m], dst=T.land[i])
+         for m in range(n)],
+        local_sem=s.read)
 
-    g.dma_start(T.y[:], T.land[:, 0:b]).then_inc(s.local, 16)
-    g.wait_ge(s.local, 48)
-    g.wait_ge(s.read, 4 * (n - 1))
+    g.wait_ge(s.arrived, 4 * n)
+    g.remote_dma_fused(
+        [RemoteDMATransfer(dst_ids=[dst_id(m) for m in range(n)], dma_engine_mask=0xFFFF, remote_sem=s.done,
+                           srcs=[T.land[k] for k in range(n)], dsts=[T.sd[i] for m in range(n)], alu_op=1)],
+        local_sem=s.read)
+
+    g.sync.wait_ge(s.done, 16 * n)
+    g.sync.dma_start(T.y[:], T.sd[:, i::n, :]).then_inc(s.stored, 16)
+    g.wait_ge(s.stored, 16)
+    g.wait_ge(s.read, 4 * n + 16)

from concourse.bass import DstId, RemoteDMATransfer

SCRATCH = {
    "xd": ("dram", [4, 128, 2], "bfloat16"),
    "land": ("dram", [4, 128, 2], "bfloat16"),
    "sd": ("dram", [4, 128, 2], "bfloat16"),
}
SEMAPHORES = ["loaded", "read", "arrived", "done", "stored"]


def rank_program(g, core, T, topo):
    rank = T.rank_of(core)
    if rank is None:
        return
    groups = T.tables["GROUPS"]
    group = [grp for grp in groups if rank in grp][0]
    n = len(group)
    i = group.index(rank)
    partner = [grp for grp in groups
               if grp is not group and topo.chip(T.cores[grp[0]]) == topo.chip(core)][0]
    s = T.sem

    def dst_id(member):
        rid, pid, _se = topo.addr(T.cores[partner[member]])
        return DstId(rid=rid, pnc=pid)

    g.sync.dma_start(T.xd[:], T.x[:]).then_inc(s.loaded, 16)
    g.wait_ge(s.loaded, 16)

    g.remote_dma_fused(
        [RemoteDMATransfer(dst_ids=[dst_id(m)], dma_engine_mask=0xF << (4 * m), remote_sem=s.arrived,
                           src=T.xd[m], dst=T.land[i])
         for m in range(n)],
        local_sem=s.read)

    g.wait_ge(s.arrived, 4 * n)
    g.remote_dma_fused(
        [RemoteDMATransfer(dst_ids=[dst_id(m) for m in range(n)], dma_engine_mask=0xFFFF, remote_sem=s.done,
                           srcs=[T.land[k] for k in range(n)], dsts=[T.sd[i] for m in range(n)], alu_op=1)],
        local_sem=s.read)

    g.sync.wait_ge(s.done, 16 * n)
    g.sync.dma_start(T.y[:], T.sd[:, i::n, :]).then_inc(s.stored, 16)
    g.wait_ge(s.stored, 16)
    g.wait_ge(s.read, 4 * n + 16)
